import numpy as np
import ml_dtypes


def mxq(x, axis, fmt="e4m3"):
    dtype, down = {"e4m3": (ml_dtypes.float8_e4m3fn, 7), "e5m2": (ml_dtypes.float8_e5m2, 14)}[fmt]
    v = np.moveaxis(np.asarray(x, np.float32).astype(ml_dtypes.bfloat16).astype(np.float64), axis, -1)
    blocks = v.reshape(v.shape[:-1] + (-1, 32))
    amax = np.abs(blocks).max(-1, keepdims=True)
    byte = np.maximum(np.where(amax > 0, np.frexp(amax)[1] - 1 + 127, 0) - down, 1)
    scale = np.exp2(byte - 127.0)
    codes = (blocks / scale).astype(np.float32).astype(dtype).astype(np.float64)
    return np.moveaxis((codes * scale).reshape(v.shape), -1, axis)


WIDE = False


def mx_kscale(k):
    if not WIDE:
        return np.ones(k)
    levels = np.array([10, -10, 5, -5, 0])
    if k % 512:
        return np.exp2(np.random.permutation(np.resize(levels, k // 32))).repeat(32)
    a = np.empty((k // 512, 16))
    for p in range(k // 512):
        a[p, :8] = np.random.permutation(np.resize(levels, 8))
        for g in range(8):
            far = levels[np.abs(levels - a[p, g]) >= 10]
            a[p, g + 8] = far[np.random.randint(len(far))]
    return np.exp2(a.ravel()).repeat(32)


BF16 = ml_dtypes.bfloat16


def bf(x):
    return np.asarray(x, np.float32).astype(BF16)


def f64(x):
    return np.asarray(x).astype(np.float64)


E2M1 = np.array([0.0, 0.5, 1.0, 1.5, 2.0, 3.0, 4.0, 6.0, -0.0, -0.5, -1.0, -1.5, -2.0, -3.0, -4.0, -6.0])


def pack_weight(w, fmt):
    k, n = w.shape
    w = f64(bf(w)).reshape(k // 32, 32, n)
    amax = np.abs(w).max(1)
    if fmt == "e4m3":
        byte = np.frexp(amax)[1] - 1 + 127 - 7
    else:
        mant, ex = np.frexp(amax / 6.0)
        byte = np.where(mant > 0.5, ex, ex - 1) + 127
    byte = np.clip(np.where(amax > 0, byte, 1), 1, 254)
    scaled = (w * np.exp2(127.0 - byte)[:, None, :]).reshape(k, n).astype(np.float32)
    by_word = np.ascontiguousarray(scaled.reshape(k // 512, 128, 4, n).transpose(0, 1, 3, 2))
    if fmt == "e4m3":
        words = by_word.astype(ml_dtypes.float8_e4m3fn).view(np.uint8)
    else:
        c = by_word.astype(ml_dtypes.float4_e2m1fn).view(np.uint8) & 0xF
        words = c[..., 0::2] | (c[..., 1::2] << 4)
    return np.ascontiguousarray(words), np.ascontiguousarray(byte.astype(np.uint8).reshape(k // 512, 16, n))


def unpack_weight(words, scales, fmt):
    g, p, n, _ = words.shape
    if fmt == "e4m3":
        vals = np.ascontiguousarray(words).view(ml_dtypes.float8_e4m3fn).astype(np.float64)
    else:
        nib = np.empty((g, p, n, 4), np.uint8)
        nib[..., 0::2] = words & 0xF
        nib[..., 1::2] = words >> 4
        vals = E2M1[nib]
    vals = vals * np.repeat(np.exp2(scales.astype(np.float64) - 127.0), 8, axis=1)[..., None]
    return vals.transpose(0, 1, 3, 2).reshape(g * 512, n)
def pack4(w):
    words, scales = pack_weight(w, "e2m1")
    return words.reshape(words.shape[0], 128, -1), scales


def unpack4(words, scales):
    return unpack_weight(words.reshape(words.shape[0], 128, -1, 2), scales, "e2m1")


T, A, N, R, Q = 2048, 1536, 1024, 512, 256


def draw0():
    s = mx_kscale(A)
    t = mx_kscale(N)
    u = mx_kscale(T)
    sens = np.random.standard_normal((N, R)) / np.sqrt(N) / t[:, None]
    sens_words, sens_scales = pack4(sens)
    return {"flow": bf(np.random.standard_normal((T, A)) * s),
            "impact": bf(np.random.standard_normal((A, N)) / np.sqrt(A) / s[:, None]),
            "vol": bf((1 + 0.2 * np.random.standard_normal(N)) * t),
            "depth": bf((1 + 0.2 * np.random.standard_normal(T)) * u),
            "sched": bf(np.random.standard_normal((Q, T)) / np.sqrt(T) / u),
            "sens_words": sens_words,
            "sens_scales": sens_scales}


def core(flow, impact, vol, depth, sched, sens_words, sens_scales):
    z = mxq(f64(flow), 1, "e4m3") @ mxq(f64(impact), 0, "e4m3")
    h = np.tanh(z)
    moves = h * f64(vol)
    hedge = mxq(moves, 1, "e4m3") @ unpack4(sens_words, sens_scales)
    weighted = h * f64(depth)[:, None]
    cost = mxq(f64(sched), 1, "e4m3") @ mxq(weighted, 0, "e4m3")
    return hedge, cost


def e4m3fn_bytes(y):
    return np.clip(np.asarray(y, np.float64), -448.0, 448.0).astype(np.float32).astype(ml_dtypes.float8_e4m3fn).view(np.uint8)


def e4m3fn_values(b):
    return np.asarray(b, np.uint8).view(ml_dtypes.float8_e4m3fn).astype(np.float64)


def setup_inputs():
    d = draw0()
    x0 = np.asarray(d['flow']).astype(np.float64)
    s = (np.max(np.abs(x0), axis=(0,), keepdims=True) / 448.0).astype(np.float32)
    out = {}
    for k, v in d.items():
        if k == 'flow':
            out['flow_bytes'] = e4m3fn_bytes(x0 / s.astype(np.float64))
            out['flow_scale'] = s
        else:
            out[k] = v
    return out


def reference(flow_bytes, flow_scale, impact, vol, depth, sched, sens_words, sens_scales):
    return core(e4m3fn_values(flow_bytes) * flow_scale.astype(np.float64), impact, vol, depth, sched, sens_words, sens_scales)

@@ -1,0 +1,420 @@
+from contextlib import ExitStack
+
+import concourse.mybir as mybir
+from concourse.masks import make_identity
+
+T, A, N, R, Q = 2048, 1536, 1024, 512, 256
+
+F32 = mybir.dt.float32
+BF16 = mybir.dt.bfloat16
+U8 = mybir.dt.uint8
+U32 = mybir.dt.uint32
+I32 = mybir.dt.int32
+FP8 = mybir.dt.float8_e4m3fn
+FP8X4 = mybir.dt.float8_e4m3fn_x4
+FP4X4 = mybir.dt.float4_e2m1fn_x4
+MULT = mybir.AluOpType.mult
+TANH = mybir.ActivationFunctionType.Tanh
+COPY = mybir.ActivationFunctionType.Copy
+
+FLOPS = 2 * T * A * N + 2 * T * N * R + 2 * Q * T * N
+
+P = 128
+PACK = 4
+K_PASS = P * PACK
+A_PASSES = A // K_PASS
+N_PASSES = N // K_PASS
+T_PASSES = T // K_PASS
+TILES = T // P
+BANK = 512
+W_LEAD = 5
+CH = 256
+CHUNKS = N // CH
+
+
+def tile_cross_impact_hedge_s8_kernel(
+    tc, flow_bytes, flow_scale, impact, vol, depth, sched, sens_words, sens_scales, hedge, cost
+):
+    nc = tc.nc
+    with ExitStack() as ctx:
+        keep = ctx.enter_context(tc.tile_pool(name="keep", bufs=1))
+        work = ctx.enter_context(tc.tile_pool(name="work", bufs=3))
+        psum = ctx.enter_context(tc.psum_pool(name="psum", bufs=2))
+        ctx.enter_context(tc.manual_schedule())
+
+        warm = keep.tile([P, 1], F32, name="warm")
+        nc.vector.memset(warm[:], 0.0)
+        nc.scalar.activation(out=warm[:], in_=warm[:], func=TANH)
+        w_scales = keep.tile([P, N_PASSES, R], U8, name="w_scales", align_bytes=64)
+        nc.vector.memset(w_scales[:].bitcast(I32), 0)
+        ident = keep.tile([P, P], F32, name="ident")
+        make_identity(nc, ident[:])
+
+        flow_view = flow_bytes.rearrange("(g p j) a -> g p j a", p=P, j=PACK)
+        flow_sb = []
+        for g in range(T_PASSES):
+            for half in range(2):
+                t_f = keep.tile([P, 2, A], U8, name=f"flow_{g}_{half}", align_bytes=64)
+                flow_sb.append(t_f)
+
+        def load_flow(pair):
+            g, half = divmod(pair, 2)
+            nc.sync.dma_start(out=flow_sb[pair][:], in_=flow_view[g, :, 2 * half : 2 * half + 2, :])
+
+        imp_view = impact.rearrange("(c p t) n -> c p t n", p=P, t=PACK)
+        imp_raw = {}
+        for c in range(A_PASSES):
+            for half in range(N_PASSES):
+                t_i = keep.tile([P, PACK, BANK], BF16, name=f"imp_raw_{c}_{half}", align_bytes=64)
+                imp_raw[c, half] = t_i
+
+        def load_impact(c, half):
+            nc.sync.dma_start(out=imp_raw[c, half][:], in_=imp_view[c, :, :, half * BANK : (half + 1) * BANK])
+
+        scale_sb = keep.tile([P, A], F32, name="scale_sb", align_bytes=64)
+        vol_b = keep.tile([P, N_PASSES, PACK], BF16, name="vol_b")
+        depth_b = keep.tile([P, T_PASSES, PACK], BF16, name="depth_b")
+        w_words = keep.tile([P, N_PASSES, 2 * R], U8, name="w_words", align_bytes=64)
+        sched_sb = []
+        for qt in range(2):
+            t_s = keep.tile([P, T], BF16, name=f"sched_{qt}", align_bytes=64)
+            sched_sb.append(t_s)
+
+        load_impact(0, 0)
+        load_impact(1, 0)
+        load_flow(0)
+        nc.sync.dma_start(out=scale_sb[:], in_=flow_scale.rearrange("o k -> (o k)").partition_broadcast(P))
+        load_impact(2, 0)
+        load_flow(1)
+        nc.scalar.dma_start(out=vol_b[:], in_=vol.rearrange("(g p j) -> p g j", p=P, j=PACK))
+        nc.scalar.dma_start(out=depth_b[:], in_=depth.rearrange("(g p j) -> p g j", p=P, j=PACK))
+        load_impact(0, 1)
+        load_impact(1, 1)
+        load_impact(2, 1)
+        load_flow(2)
+        for q4 in range(4):
+            nc.sync.dma_start(
+                out=w_scales[32 * q4 : 32 * q4 + 4, :, :].bitcast(I32),
+                in_=sens_scales[:, 4 * q4 : 4 * q4 + 4, :].rearrange("g r n -> r g n").bitcast(I32),
+            )
+        nc.sync.dma_start(out=w_words[:].bitcast(I32), in_=sens_words.rearrange("g p b -> p g b").bitcast(I32))
+        load_flow(3)
+        load_flow(4)
+        for qt in range(2):
+            nc.sync.dma_start(out=sched_sb[qt][:], in_=sched[qt * P : (qt + 1) * P, :])
+        load_flow(5)
+        load_flow(6)
+        load_flow(7)
+
+        vol_f = keep.tile([P, N_PASSES, PACK], F32, name="vol_f")
+        depth_f = keep.tile([P, T_PASSES, PACK], F32, name="depth_f")
+
+        imp_codes = keep.tile([P, A_PASSES, N], U32, name="imp_codes", align_bytes=64)
+        imp_scales = keep.tile([P, A_PASSES, N], U8, name="imp_scales", align_bytes=64)
+        wt_codes = keep.tile([P, T_PASSES, N], U32, name="wt_codes", align_bytes=64)
+        wt_scales = keep.tile([P, T_PASSES, N], U8, name="wt_scales", align_bytes=64)
+        sch_codes = keep.tile([P, 2, T_PASSES, P], U32, name="sch_codes", align_bytes=64)
+        sch_scales = keep.tile([P, 2, T_PASSES, P], U8, name="sch_scales", align_bytes=64)
+        tiles = {}
+
+        def impact_interleave(c, half, engine):
+            grouped = work.tile([P, BANK, PACK], BF16, name=f"imp_grp_{c}_{half}", tag="imp_grp", bufs=3, align_bytes=64)
+            tiles["ig", c, half] = grouped
+            dst = grouped[:].rearrange("p (j m) t -> p j m t", j=PACK)
+            src = imp_raw[c, half][:].rearrange("p t (m j) -> p j m t", j=PACK)
+            if engine == "A":
+                nc.scalar.copy(out=dst, in_=src)
+            else:
+                nc.vector.tensor_copy(out=dst, in_=src)
+
+        def impact_quantize(c, half):
+            cols = slice(half * BANK, (half + 1) * BANK)
+            nc.vector.quantize_mx(
+                out=imp_codes[:, c, cols].bitcast(FP8X4),
+                scales=imp_scales[:, c, cols],
+                in_=tiles.pop(("ig", c, half))[:].rearrange("p n t -> p (n t)"),
+            )
+
+        def widen(i):
+            wide = work.tile([P, A], BF16, name=f"wide_{i}", tag="wide", bufs=W_LEAD + 2, align_bytes=64)
+            tiles["wide", i] = wide
+            nc.vector.tensor_tensor(
+                out=wide[:], in0=flow_sb[i // 2][:, i % 2, :].bitcast(FP8), in1=scale_sb[:], op=MULT
+            )
+
+        def flow_transpose(i):
+            words = tiles.pop(("wide", i))[:].bitcast(F32)
+            for part, passes in ((0, (0, 1)), (1, (2,))):
+                bank = psum.tile([P, PACK, P], F32, name=f"xt_{i}_{part}", tag="xt", bufs=3)
+                tiles["xt", i, part] = bank
+                slot = 0
+                for c in passes:
+                    for u in range(2):
+                        nc.tensor.transpose(
+                            bank[:, slot, :], words[:, 256 * c + u : 256 * (c + 1) : 2], ident[:]
+                        )
+                        slot += 1
+
+        def flow_exit(i):
+            grouped = work.tile([P, A_PASSES, P, PACK], BF16, name=f"fg_{i}", tag="fg", bufs=3, align_bytes=64)
+            tiles["fg", i] = grouped
+            words = grouped[:].rearrange("p c r t -> p (c r t)").bitcast(F32)
+            words = words.rearrange("p (c r u) -> p c r u", c=A_PASSES, u=2)
+            xt0 = tiles.pop(("xt", i, 0))
+            xt1 = tiles.pop(("xt", i, 1))
+            nc.scalar.copy(out=words[:, 0:2, :, :], in_=xt0[:].rearrange("p (c u) r -> p c r u", u=2))
+            nc.scalar.copy(out=words[:, 2, :, :], in_=xt1[:, 0:2, :].rearrange("p u r -> p r u"))
+
+        def flow_quantize(i):
+            codes = work.tile([P, A_PASSES, P], U32, name=f"fc_{i}", tag="fc", bufs=3, align_bytes=64)
+            scales = work.tile([P, A_PASSES, P], U8, name=f"fs_{i}", tag="fs", bufs=3, align_bytes=64)
+            tiles["fc", i] = (codes, scales)
+            grouped = tiles.pop(("fg", i))
+            for lo, hi in ((0, 2), (2, 3)):
+                nc.vector.quantize_mx(
+                    out=codes[:, lo:hi, :].rearrange("p c r -> p (c r)").bitcast(FP8X4),
+                    scales=scales[:, lo:hi, :].rearrange("p c r -> p (c r)"),
+                    in_=grouped[:, lo:hi, :, :].rearrange("p c r t -> p (c r t)"),
+                )
+
+        def impact_matmul(i, half):
+            codes, scales = tiles["fc", i]
+            z = psum.tile([P, BANK], F32, name=f"z_{i}_{half}", tag="z", bufs=2)
+            tiles["z", i, half] = z
+            cols = slice(half * BANK, (half + 1) * BANK)
+            for c in range(A_PASSES):
+                nc.tensor.matmul_mx(
+                    out=z[:],
+                    lhsT=codes[:, c, :].bitcast(FP8X4),
+                    lhsT_scale=scales[:, c, :],
+                    rhs=imp_codes[:, c, cols].bitcast(FP8X4),
+                    rhs_scale=imp_scales[:, c, cols],
+                    start=(c == 0),
+                    stop=(c == A_PASSES - 1),
+                )
+
+        def saturate(i, half):
+            if half == 0:
+                h = work.tile([P, N], F32, name=f"h_{i}", tag="h", bufs=4, align_bytes=64)
+                tiles["h", i] = h
+            h = tiles["h", i]
+            nc.scalar.activation(out=h[:, half * BANK : (half + 1) * BANK], in_=tiles.pop(("z", i, half))[:], func=TANH)
+
+        def weigh(i, engine):
+            g, j = divmod(i, PACK)
+            if j == 0:
+                planes = work.tile([P, PACK, N], BF16, name=f"wp_{g}", tag="wp", bufs=2, align_bytes=64)
+                tiles["wp", g] = planes
+            planes = tiles["wp", g]
+            if engine == "A":
+                nc.scalar.activation(
+                    out=planes[:, j, :], in_=tiles["h", i][:], func=COPY, scale=depth_f[:, g, j : j + 1]
+                )
+            else:
+                nc.vector.tensor_scalar(
+                    out=planes[:, j, :], in0=tiles["h", i][:], scalar1=depth_f[:, g, j : j + 1], scalar2=None, op0=MULT
+                )
+
+        def weighted_interleave(g, ch, engine):
+            grouped = work.tile([P, CH, PACK], BF16, name=f"wg_{g}_{ch}", tag="wg", bufs=4, align_bytes=64)
+            tiles["wg", g, ch] = grouped
+            src = tiles["wp", g][:, :, ch * CH : (ch + 1) * CH].rearrange("p j n -> p n j")
+            if engine == "A":
+                nc.scalar.copy(out=grouped[:], in_=src)
+            else:
+                nc.vector.tensor_copy(out=grouped[:], in_=src)
+
+        def weighted_quantize(g, ch):
+            cols = slice(ch * CH, (ch + 1) * CH)
+            nc.vector.quantize_mx(
+                out=wt_codes[:, g, cols].bitcast(FP8X4),
+                scales=wt_scales[:, g, cols],
+                in_=tiles.pop(("wg", g, ch))[:].rearrange("p n t -> p (n t)"),
+            )
+
+        def moves_transpose(i, half):
+            bank = psum.tile([P, PACK, P], F32, name=f"ht_{i}_{half}", tag="ht", bufs=2)
+            tiles["ht", i, half] = bank
+            h = tiles["h", i]
+            for j in range(PACK):
+                c0 = half * BANK + j * P
+                nc.tensor.transpose(bank[:, j, :], h[:, c0 : c0 + P], ident[:])
+
+        def moves_scale(i, half):
+            if half == 0:
+                grouped = work.tile([P, N_PASSES, P, PACK], BF16, name=f"mg_{i}", tag="mg", bufs=3, align_bytes=64)
+                tiles["mg", i] = grouped
+            grouped = tiles["mg", i]
+            nc.vector.tensor_tensor(
+                out=grouped[:, half, :, :],
+                in0=tiles.pop(("ht", i, half))[:].rearrange("p j t -> p t j"),
+                in1=vol_f[:, half, :].unsqueeze(1).to_broadcast([P, P, PACK]),
+                op=MULT,
+            )
+
+        def moves_quantize(i):
+            codes = work.tile([P, N_PASSES, P], U32, name=f"mc_{i}", tag="mc", bufs=4, align_bytes=64)
+            scales = work.tile([P, N_PASSES, P], U8, name=f"ms_{i}", tag="ms", bufs=4, align_bytes=64)
+            tiles["mc", i] = (codes, scales)
+            nc.vector.quantize_mx(
+                out=codes[:].rearrange("p g t -> p (g t)").bitcast(FP8X4),
+                scales=scales[:].rearrange("p g t -> p (g t)"),
+                in_=tiles.pop(("mg", i))[:].rearrange("p g t j -> p (g t j)"),
+            )
+
+        def hedge_matmul(i):
+            codes, scales = tiles.pop(("mc", i))
+            bank = psum.tile([P, R], F32, name=f"hg_{i}", tag="hg", bufs=1)
+            tiles["hg", i] = bank
+            for g in range(N_PASSES):
+                nc.tensor.matmul_mx(
+                    out=bank[:],
+                    lhsT=codes[:, g, :].bitcast(FP8X4),
+                    lhsT_scale=scales[:, g, :],
+                    rhs=w_words[:, g, :].bitcast(FP4X4),
+                    rhs_scale=w_scales[:, g, :],
+                    start=(g == 0),
+                    stop=(g == N_PASSES - 1),
+                )
+
+        hedge_view = hedge.rearrange("(g p j) r -> g j p r", p=P, j=PACK)
+
+        def hedge_exit(i, engine):
+            g, j = divmod(i, PACK)
+            res = work.tile([P, R], F32, name=f"hr_{i}", tag="hr", bufs=3, align_bytes=64)
+            bank = tiles.pop(("hg", i))
+            if engine == "A":
+                nc.scalar.copy(out=res[:], in_=bank[:])
+            else:
+                nc.vector.tensor_copy(out=res[:], in_=bank[:])
+            nc.sync.dma_start(out=hedge_view[g, j], in_=res[:])
+
+        def sched_transpose(b):
+            qt, gp = divmod(b, 2)
+            words = sched_sb[qt][:].bitcast(F32)
+            bank = psum.tile([P, PACK, P], F32, name=f"st_{b}", tag="xt", bufs=3)
+            tiles["st", b] = bank
+            for s in range(2):
+                g = 2 * gp + s
+                for u in range(2):
+                    nc.tensor.transpose(bank[:, 2 * s + u, :], words[:, 256 * g + u : 256 * (g + 1) : 2], ident[:])
+
+        def sched_exit(b):
+            grouped = work.tile([P, 2, P, PACK], BF16, name=f"sg_{b}", tag="sg", bufs=2, align_bytes=64)
+            tiles["sg", b] = grouped
+            words = grouped[:].rearrange("p s q t -> p (s q t)").bitcast(F32)
+            nc.scalar.copy(
+                out=words.rearrange("p (s q u) -> p s q u", s=2, u=2),
+                in_=tiles.pop(("st", b))[:].rearrange("p (s u) q -> p s q u", u=2),
+            )
+
+        def sched_quantize(b):
+            qt, gp = divmod(b, 2)
+            nc.vector.quantize_mx(
+                out=sch_codes[:, qt, 2 * gp : 2 * gp + 2, :].rearrange("p s q -> p (s q)").bitcast(FP8X4),
+                scales=sch_scales[:, qt, 2 * gp : 2 * gp + 2, :].rearrange("p s q -> p (s q)"),
+                in_=tiles.pop(("sg", b))[:].rearrange("p s q t -> p (s q t)"),
+            )
+
+        def cost_matmul(qt, half, g):
+            if g == 0:
+                bank = psum.tile(
+                    [P, BANK], F32, name=f"cost_{qt}_{half}", tag="xt" if half == 0 else "z", bufs=3 if half == 0 else 2
+                )
+                tiles["cb", qt, half] = bank
+            cols = slice(half * BANK, (half + 1) * BANK)
+            nc.tensor.matmul_mx(
+                out=tiles["cb", qt, half][:],
+                lhsT=sch_codes[:, qt, g, :].bitcast(FP8X4),
+                lhsT_scale=sch_scales[:, qt, g, :],
+                rhs=wt_codes[:, g, cols].bitcast(FP8X4),
+                rhs_scale=wt_scales[:, g, cols],
+                start=(g == 0),
+                stop=(g == T_PASSES - 1),
+            )
+
+        def cost_exit(qt, half, engine):
+            res = work.tile([P, BANK], F32, name=f"cr_{qt}_{half}", tag="cr", bufs=4, align_bytes=64)
+            dst = res[:].rearrange("p (m j) -> p m j", j=PACK)
+            src = tiles.pop(("cb", qt, half))[:].rearrange("p (j m) -> p m j", j=PACK)
+            if engine == "A":
+                nc.scalar.copy(out=dst, in_=src)
+            else:
+                nc.vector.tensor_copy(out=dst, in_=src)
+            nc.sync.dma_start(out=cost[qt * P : (qt + 1) * P, half * BANK : (half + 1) * BANK], in_=res[:])
+
+        impact_interleave(0, 0, "A")
+        impact_interleave(1, 0, "D")
+        nc.vector.tensor_copy(out=vol_f[:], in_=vol_b[:])
+        nc.vector.tensor_copy(out=depth_f[:], in_=depth_b[:])
+        impact_quantize(0, 0)
+        impact_interleave(2, 0, "A")
+        widen(0)
+        impact_quantize(1, 0)
+        widen(1)
+        flow_transpose(0)
+        flow_exit(0)
+        impact_quantize(2, 0)
+        impact_interleave(0, 1, "A")
+        flow_quantize(0)
+        widen(2)
+        flow_transpose(1)
+        impact_interleave(1, 1, "D")
+        flow_exit(1)
+        impact_quantize(0, 1)
+        impact_interleave(2, 1, "A")
+        impact_quantize(1, 1)
+        widen(3)
+        impact_quantize(2, 1)
+        widen(4)
+        flow_quantize(1)
+
+        for s in range(TILES + 3):
+            if s + W_LEAD < TILES:
+                widen(s + W_LEAD)
+            if s + 1 < TILES and s > 0:
+                flow_transpose(s + 1)
+                flow_exit(s + 1)
+            if 2 <= s < 6:
+                sched_transpose(s - 2)
+                sched_exit(s - 2)
+            if 0 <= s - 1 < TILES:
+                for half in range(N_PASSES):
+                    moves_transpose(s - 1, half)
+                    moves_scale(s - 1, half)
+            g, ch = divmod(s - 4, CHUNKS)
+            inter = s >= 4 and g < T_PASSES - 1
+            if inter:
+                weighted_interleave(g, ch, "D")
+            if 0 <= s - 1 < TILES:
+                moves_quantize(s - 1)
+            if 2 <= s < 6:
+                sched_quantize(s - 2)
+            if s + 1 < TILES and s > 0:
+                flow_quantize(s + 1)
+            if inter:
+                weighted_quantize(g, ch)
+            if 0 <= s - 2 < TILES:
+                hedge_matmul(s - 2)
+                hedge_exit(s - 2, "A")
+            if s == TILES - 1:
+                for g in range(T_PASSES - 1):
+                    for qt in range(2):
+                        cost_matmul(qt, 0, g)
+            if s < TILES:
+                for half in range(N_PASSES):
+                    impact_matmul(s, half)
+                    saturate(s, half)
+                weigh(s, "A" if s < TILES - 1 else "D")
+            if s == TILES:
+                for g in range(T_PASSES - 1):
+                    for qt in range(2):
+                        cost_matmul(qt, 1, g)
+                for ch in range(CHUNKS):
+                    weighted_interleave(T_PASSES - 1, ch, "D" if ch % 2 == 0 else "A")
+                for ch in range(CHUNKS):
+                    weighted_quantize(T_PASSES - 1, ch)
+                for half in range(N_PASSES):
+                    for qt in range(2):
+                        cost_matmul(qt, half, T_PASSES - 1)
+                        cost_exit(qt, half, "A" if qt == 0 else "D")

@@ -27,7 +27,7 @@ N_PASSES = N // K_PASS
 T_PASSES = T // K_PASS
 TILES = T // P
 BANK = 512
-W_LEAD = 5
+W_LEAD = 2
 CH = 256
 CHUNKS = N // CH
 
@@ -45,10 +45,14 @@ def tile_cross_impact_hedge_s8_kernel(
         warm = keep.tile([P, 1], F32, name="warm")
         nc.vector.memset(warm[:], 0.0)
         nc.scalar.activation(out=warm[:], in_=warm[:], func=TANH)
+        scale_rows = keep.tile([P, 3 * P], F32, name="scale_rows")
+        nc.vector.memset(scale_rows[:], 0.0)
         w_scales = keep.tile([P, N_PASSES, R], U8, name="w_scales", align_bytes=64)
         nc.vector.memset(w_scales[:].bitcast(I32), 0)
         ident = keep.tile([P, P], F32, name="ident")
         make_identity(nc, ident[:])
+        ident_b = keep.tile([P, P], BF16, name="ident_b")
+        make_identity(nc, ident_b[:])
 
         flow_view = flow_bytes.rearrange("(g p j) a -> g p j a", p=P, j=PACK)
         flow_sb = []
@@ -80,18 +84,18 @@ def tile_cross_impact_hedge_s8_kernel(
             t_s = keep.tile([P, T], BF16, name=f"sched_{qt}", align_bytes=64)
             sched_sb.append(t_s)
 
+        nc.sync.dma_start(out=scale_rows[0:4, :], in_=flow_scale.rearrange("o (r k) -> (o r) k", r=4))
         load_impact(0, 0)
         load_impact(1, 0)
         load_flow(0)
-        nc.sync.dma_start(out=scale_sb[:], in_=flow_scale.rearrange("o k -> (o k)").partition_broadcast(P))
         load_impact(2, 0)
-        load_flow(1)
-        nc.scalar.dma_start(out=vol_b[:], in_=vol.rearrange("(g p j) -> p g j", p=P, j=PACK))
-        nc.scalar.dma_start(out=depth_b[:], in_=depth.rearrange("(g p j) -> p g j", p=P, j=PACK))
         load_impact(0, 1)
         load_impact(1, 1)
         load_impact(2, 1)
+        load_flow(1)
         load_flow(2)
+        nc.sync.dma_start(out=vol_b[:], in_=vol.rearrange("(g p j) -> p g j", p=P, j=PACK))
+        nc.sync.dma_start(out=depth_b[:], in_=depth.rearrange("(g p j) -> p g j", p=P, j=PACK))
         for q4 in range(4):
             nc.sync.dma_start(
                 out=w_scales[32 * q4 : 32 * q4 + 4, :, :].bitcast(I32),
@@ -127,6 +131,26 @@ def tile_cross_impact_hedge_s8_kernel(
             else:
                 nc.vector.tensor_copy(out=dst, in_=src)
 
+        def impact_pass(c, half, b):
+            bank = psum.tile([P, 2, P, PACK], BF16, name=f"ip_{c}_{half}_{b}", tag="xt", bufs=3)
+            tiles["ip", c, half, b] = bank
+            src = imp_raw[c, half][:].rearrange("p t (m j) -> p j m t", j=PACK)
+            for s in range(2):
+                nc.tensor.matmul(bank[:, s, :, :], lhsT=ident_b[:], rhs=src[:, 2 * b + s, :, :], start=True, stop=True)
+
+        def impact_exit(c, half, b, engine):
+            if b == 0:
+                grouped = work.tile(
+                    [P, BANK, PACK], BF16, name=f"imp_grp_{c}_{half}", tag="imp_grp", bufs=3, align_bytes=64
+                )
+                tiles["ig", c, half] = grouped
+            dst = tiles["ig", c, half][:, 2 * P * b : 2 * P * (b + 1), :].rearrange("p n t -> p (n t)")
+            src = tiles.pop(("ip", c, half, b))[:].rearrange("p s m t -> p (s m t)")
+            if engine == "A":
+                nc.scalar.copy(out=dst, in_=src)
+            else:
+                nc.vector.tensor_copy(out=dst, in_=src)
+
         def impact_quantize(c, half):
             cols = slice(half * BANK, (half + 1) * BANK)
             nc.vector.quantize_mx(
@@ -135,8 +159,25 @@ def tile_cross_impact_hedge_s8_kernel(
                 in_=tiles.pop(("ig", c, half))[:].rearrange("p n t -> p (n t)"),
             )
 
+        def spread_scale():
+            bank = psum.tile([P, 3, P], F32, name="scale_cols", tag="ht", bufs=2)
+            for b in range(3):
+                nc.tensor.transpose(bank[:, b, :], scale_rows[:, b * P : (b + 1) * P], ident[:])
+            scale_cols = keep.tile([P, 4, 3], F32, name="scale_cols_sb")
+            nc.scalar.copy(out=scale_cols[:], in_=bank[:, :, 0:4].rearrange("p b r -> p r b"))
+            for c in range(A_PASSES):
+                bank = psum.tile([P, PACK, P], F32, name=f"scale_bank_{c}", tag="z", bufs=2)
+                for s in range(PACK):
+                    k = PACK * c + s
+                    nc.tensor.transpose(
+                        bank[:, s, :], scale_cols[:, k // 3, k % 3 : k % 3 + 1].to_broadcast([P, P]), ident[:]
+                    )
+                nc.scalar.copy(
+                    out=scale_sb[:, c * K_PASS : (c + 1) * K_PASS], in_=bank[:].rearrange("p s k -> p (s k)")
+                )
+
         def widen(i):
-            wide = work.tile([P, A], BF16, name=f"wide_{i}", tag="wide", bufs=W_LEAD + 2, align_bytes=64)
+            wide = work.tile([P, A], BF16, name=f"wide_{i}", tag="wide", bufs=4, align_bytes=64)
             tiles["wide", i] = wide
             nc.vector.tensor_tensor(
                 out=wide[:], in0=flow_sb[i // 2][:, i % 2, :].bitcast(FP8), in1=scale_sb[:], op=MULT
@@ -200,19 +241,19 @@ def tile_cross_impact_hedge_s8_kernel(
             h = tiles["h", i]
             nc.scalar.activation(out=h[:, half * BANK : (half + 1) * BANK], in_=tiles.pop(("z", i, half))[:], func=TANH)
 
-        def weigh(i, engine):
+        def weigh(i, engine, lo=0, hi=N):
             g, j = divmod(i, PACK)
             if j == 0:
-                planes = work.tile([P, PACK, N], BF16, name=f"wp_{g}", tag="wp", bufs=2, align_bytes=64)
+                planes = work.tile([P, PACK, N], BF16, name=f"wp_{g}", tag="wp", bufs=3, align_bytes=64)
                 tiles["wp", g] = planes
             planes = tiles["wp", g]
             if engine == "A":
                 nc.scalar.activation(
-                    out=planes[:, j, :], in_=tiles["h", i][:], func=COPY, scale=depth_f[:, g, j : j + 1]
+                    out=planes[:, j, lo:hi], in_=tiles["h", i][:, lo:hi], func=COPY, scale=depth_f[:, g, j : j + 1]
                 )
             else:
                 nc.vector.tensor_scalar(
-                    out=planes[:, j, :], in0=tiles["h", i][:], scalar1=depth_f[:, g, j : j + 1], scalar2=None, op0=MULT
+                    out=planes[:, j, lo:hi], in0=tiles["h", i][:, lo:hi], scalar1=depth_f[:, g, j : j + 1], scalar2=None, op0=MULT
                 )
 
         def weighted_interleave(g, ch, engine):
@@ -223,6 +264,29 @@ def tile_cross_impact_hedge_s8_kernel(
                 nc.scalar.copy(out=grouped[:], in_=src)
             else:
                 nc.vector.tensor_copy(out=grouped[:], in_=src)
+
+        def weighted_pass(g, ch, tag="xt", bufs=3):
+            bank = psum.tile([P, 2, P, PACK], BF16, name=f"wq_{g}_{ch}", tag=tag, bufs=bufs)
+            tiles["wb", g, ch] = bank
+            for s in range(2):
+                c0 = ch * CH + s * P
+                nc.tensor.matmul(
+                    bank[:, s, :, :],
+                    lhsT=ident_b[:],
+                    rhs=tiles["wp", g][:, :, c0 : c0 + P].rearrange("p j n -> p n j"),
+                    start=True,
+                    stop=True,
+                )
+
+        def weighted_exit(g, ch, engine):
+            grouped = work.tile([P, CH, PACK], BF16, name=f"wg_{g}_{ch}", tag="wg", bufs=4, align_bytes=64)
+            tiles["wg", g, ch] = grouped
+            dst = grouped[:].rearrange("p n j -> p (n j)")
+            src = tiles.pop(("wb", g, ch))[:].rearrange("p s n j -> p (s n j)")
+            if engine == "A":
+                nc.scalar.copy(out=dst, in_=src)
+            else:
+                nc.vector.tensor_copy(out=dst, in_=src)
 
         def weighted_quantize(g, ch):
             cols = slice(ch * CH, (ch + 1) * CH)
@@ -343,78 +407,109 @@ def tile_cross_impact_hedge_s8_kernel(
                 nc.vector.tensor_copy(out=dst, in_=src)
             nc.sync.dma_start(out=cost[qt * P : (qt + 1) * P, half * BANK : (half + 1) * BANK], in_=res[:])
 
-        impact_interleave(0, 0, "A")
-        impact_interleave(1, 0, "D")
-        nc.vector.tensor_copy(out=vol_f[:], in_=vol_b[:])
-        nc.vector.tensor_copy(out=depth_f[:], in_=depth_b[:])
-        impact_quantize(0, 0)
-        impact_interleave(2, 0, "A")
+        def impact_by_pe(c, half):
+            for b in range(2):
+                impact_pass(c, half, b)
+                impact_exit(c, half, b, "A")
+
+        spread_scale()
+        impact_interleave(0, 0, "D")
+        impact_by_pe(1, 0)
         widen(0)
-        impact_quantize(1, 0)
-        widen(1)
+        impact_quantize(0, 0)
+        impact_by_pe(2, 0)
         flow_transpose(0)
         flow_exit(0)
+        impact_quantize(1, 0)
+        impact_by_pe(0, 1)
+        widen(1)
         impact_quantize(2, 0)
-        impact_interleave(0, 1, "A")
         flow_quantize(0)
-        widen(2)
+        impact_by_pe(1, 1)
         flow_transpose(1)
-        impact_interleave(1, 1, "D")
         flow_exit(1)
         impact_quantize(0, 1)
-        impact_interleave(2, 1, "A")
+        impact_matmul(0, 0)
+        saturate(0, 0)
+        impact_by_pe(2, 1)
         impact_quantize(1, 1)
-        widen(3)
-        impact_quantize(2, 1)
-        widen(4)
+        widen(2)
         flow_quantize(1)
+        impact_quantize(2, 1)
+        nc.vector.tensor_copy(out=vol_f[:], in_=vol_b[:])
+        nc.vector.tensor_copy(out=depth_f[:], in_=depth_b[:])
+        impact_matmul(0, 1)
+        saturate(0, 1)
 
-        for s in range(TILES + 3):
+        for s in range(1, TILES):
+            g, ch = divmod(s - PACK, CHUNKS)
             if s + W_LEAD < TILES:
                 widen(s + W_LEAD)
-            if s + 1 < TILES and s > 0:
+            if s >= 3:
+                hedge_exit(s - 3, "A")
+            if s + 1 < TILES:
                 flow_transpose(s + 1)
                 flow_exit(s + 1)
-            if 2 <= s < 6:
-                sched_transpose(s - 2)
-                sched_exit(s - 2)
-            if 0 <= s - 1 < TILES:
-                for half in range(N_PASSES):
-                    moves_transpose(s - 1, half)
-                    moves_scale(s - 1, half)
-            g, ch = divmod(s - 4, CHUNKS)
-            inter = s >= 4 and g < T_PASSES - 1
-            if inter:
-                weighted_interleave(g, ch, "D")
-            if 0 <= s - 1 < TILES:
-                moves_quantize(s - 1)
-            if 2 <= s < 6:
-                sched_quantize(s - 2)
-            if s + 1 < TILES and s > 0:
+            weigh(s - 1, "A")
+            if 3 <= s < 7:
+                sched_transpose(s - 3)
+                sched_exit(s - 3)
+            for half in range(N_PASSES):
+                moves_transpose(s - 1, half)
+                moves_scale(s - 1, half)
+            if s + 1 < TILES:
                 flow_quantize(s + 1)
-            if inter:
-                weighted_quantize(g, ch)
-            if 0 <= s - 2 < TILES:
+            if s >= PACK:
+                if ch % 2 == 1:
+                    weighted_pass(g, ch)
+                    weighted_exit(g, ch, "A")
+                else:
+                    weighted_interleave(g, ch, "D")
+            moves_quantize(s - 1)
+            if 3 <= s < 7:
+                sched_quantize(s - 3)
+            if s >= 2:
                 hedge_matmul(s - 2)
-                hedge_exit(s - 2, "A")
+            if s >= PACK:
+                weighted_quantize(g, ch)
             if s == TILES - 1:
-                for g in range(T_PASSES - 1):
+                for g2 in range(T_PASSES - 1):
                     for qt in range(2):
-                        cost_matmul(qt, 0, g)
-            if s < TILES:
-                for half in range(N_PASSES):
-                    impact_matmul(s, half)
-                    saturate(s, half)
-                weigh(s, "A" if s < TILES - 1 else "D")
-            if s == TILES:
-                for g in range(T_PASSES - 1):
-                    for qt in range(2):
-                        cost_matmul(qt, 1, g)
-                for ch in range(CHUNKS):
-                    weighted_interleave(T_PASSES - 1, ch, "D" if ch % 2 == 0 else "A")
-                for ch in range(CHUNKS):
-                    weighted_quantize(T_PASSES - 1, ch)
-                for half in range(N_PASSES):
-                    for qt in range(2):
-                        cost_matmul(qt, half, T_PASSES - 1)
-                        cost_exit(qt, half, "A" if qt == 0 else "D")
+                        cost_matmul(qt, 0, g2)
+            for half in range(N_PASSES):
+                impact_matmul(s, half)
+                saturate(s, half)
+
+        last = TILES - 1
+        g = T_PASSES - 1
+        weigh(last, "D", 0, BANK)
+        hedge_exit(last - 2, "A")
+        moves_transpose(last, 0)
+        weighted_interleave(g, 0, "D")
+        weighted_pass(g, 1)
+        weighted_exit(g, 1, "A")
+        moves_scale(last, 0)
+        weigh(last, "D", BANK, N)
+        moves_transpose(last, 1)
+        hedge_matmul(last - 1)
+        weighted_quantize(g, 0)
+        moves_scale(last, 1)
+        hedge_exit(last - 1, "A")
+        for g2 in range(T_PASSES - 1):
+            for qt in range(2):
+                cost_matmul(qt, 1, g2)
+        weighted_quantize(g, 1)
+        weighted_interleave(g, 2, "D")
+        weighted_pass(g, 3, "ht", 2)
+        weighted_exit(g, 3, "A")
+        moves_quantize(last)
+        for qt in range(2):
+            cost_matmul(qt, 0, g)
+            cost_exit(qt, 0, "A")
+        hedge_matmul(last)
+        hedge_exit(last, "A")
+        weighted_quantize(g, 2)
+        weighted_quantize(g, 3)
+        for qt in range(2):
+            cost_matmul(qt, 1, g)
+            cost_exit(qt, 1, "A" if qt == 0 else "D")

@@ -27,7 +27,7 @@ N_PASSES = N // K_PASS
 T_PASSES = T // K_PASS
 TILES = T // P
 BANK = 512
-W_LEAD = 2
+W_LEAD = 4
 CH = 256
 CHUNKS = N // CH
 
@@ -51,8 +51,6 @@ def tile_cross_impact_hedge_s8_kernel(
         nc.vector.memset(w_scales[:].bitcast(I32), 0)
         ident = keep.tile([P, P], F32, name="ident")
         make_identity(nc, ident[:])
-        ident_b = keep.tile([P, P], BF16, name="ident_b")
-        make_identity(nc, ident_b[:])
 
         flow_view = flow_bytes.rearrange("(g p j) a -> g p j a", p=P, j=PACK)
         flow_sb = []
@@ -124,28 +122,8 @@ def tile_cross_impact_hedge_s8_kernel(
         def impact_interleave(c, half, engine):
             grouped = work.tile([P, BANK, PACK], BF16, name=f"imp_grp_{c}_{half}", tag="imp_grp", bufs=3, align_bytes=64)
             tiles["ig", c, half] = grouped
-            dst = grouped[:].rearrange("p (j m) t -> p j m t", j=PACK)
-            src = imp_raw[c, half][:].rearrange("p t (m j) -> p j m t", j=PACK)
-            if engine == "A":
-                nc.scalar.copy(out=dst, in_=src)
-            else:
-                nc.vector.tensor_copy(out=dst, in_=src)
-
-        def impact_pass(c, half, b):
-            bank = psum.tile([P, 2, P, PACK], BF16, name=f"ip_{c}_{half}_{b}", tag="xt", bufs=3)
-            tiles["ip", c, half, b] = bank
-            src = imp_raw[c, half][:].rearrange("p t (m j) -> p j m t", j=PACK)
-            for s in range(2):
-                nc.tensor.matmul(bank[:, s, :, :], lhsT=ident_b[:], rhs=src[:, 2 * b + s, :, :], start=True, stop=True)
-
-        def impact_exit(c, half, b, engine):
-            if b == 0:
-                grouped = work.tile(
-                    [P, BANK, PACK], BF16, name=f"imp_grp_{c}_{half}", tag="imp_grp", bufs=3, align_bytes=64
-                )
-                tiles["ig", c, half] = grouped
-            dst = tiles["ig", c, half][:, 2 * P * b : 2 * P * (b + 1), :].rearrange("p n t -> p (n t)")
-            src = tiles.pop(("ip", c, half, b))[:].rearrange("p s m t -> p (s m t)")
+            dst = grouped[:].rearrange("p (n i) t -> p n t i", i=4)
+            src = imp_raw[c, half][:].rearrange("p t (n i) -> p n t i", i=4)
             if engine == "A":
                 nc.scalar.copy(out=dst, in_=src)
             else:
@@ -177,7 +155,7 @@ def tile_cross_impact_hedge_s8_kernel(
                 )
 
         def widen(i):
-            wide = work.tile([P, A], BF16, name=f"wide_{i}", tag="wide", bufs=4, align_bytes=64)
+            wide = work.tile([P, A], BF16, name=f"wide_{i}", tag="wide", bufs=5, align_bytes=64)
             tiles["wide", i] = wide
             nc.vector.tensor_tensor(
                 out=wide[:], in0=flow_sb[i // 2][:, i % 2, :].bitcast(FP8), in1=scale_sb[:], op=MULT
@@ -207,8 +185,8 @@ def tile_cross_impact_hedge_s8_kernel(
             nc.scalar.copy(out=words[:, 2, :, :], in_=xt1[:, 0:2, :].rearrange("p u r -> p r u"))
 
         def flow_quantize(i):
-            codes = work.tile([P, A_PASSES, P], U32, name=f"fc_{i}", tag="fc", bufs=3, align_bytes=64)
-            scales = work.tile([P, A_PASSES, P], U8, name=f"fs_{i}", tag="fs", bufs=3, align_bytes=64)
+            codes = work.tile([P, A_PASSES, P], U32, name=f"fc_{i}", tag="fc", bufs=4, align_bytes=64)
+            scales = work.tile([P, A_PASSES, P], U8, name=f"fs_{i}", tag="fs", bufs=4, align_bytes=64)
             tiles["fc", i] = (codes, scales)
             grouped = tiles.pop(("fg", i))
             for lo, hi in ((0, 2), (2, 3)):
@@ -238,8 +216,11 @@ def tile_cross_impact_hedge_s8_kernel(
             if half == 0:
                 h = work.tile([P, N], F32, name=f"h_{i}", tag="h", bufs=4, align_bytes=64)
                 tiles["h", i] = h
-            h = tiles["h", i]
-            nc.scalar.activation(out=h[:, half * BANK : (half + 1) * BANK], in_=tiles.pop(("z", i, half))[:], func=TANH)
+            nc.scalar.activation(
+                out=tiles["h", i][:, half * BANK : (half + 1) * BANK].rearrange("p (j m) -> p j m", j=PACK),
+                in_=tiles.pop(("z", i, half))[:].rearrange("p (m j) -> p j m", j=PACK),
+                func=TANH,
+            )
 
         def weigh(i, engine, lo=0, hi=N):
             g, j = divmod(i, PACK)
@@ -259,30 +240,8 @@ def tile_cross_impact_hedge_s8_kernel(
         def weighted_interleave(g, ch, engine):
             grouped = work.tile([P, CH, PACK], BF16, name=f"wg_{g}_{ch}", tag="wg", bufs=4, align_bytes=64)
             tiles["wg", g, ch] = grouped
-            src = tiles["wp", g][:, :, ch * CH : (ch + 1) * CH].rearrange("p j n -> p n j")
-            if engine == "A":
-                nc.scalar.copy(out=grouped[:], in_=src)
-            else:
-                nc.vector.tensor_copy(out=grouped[:], in_=src)
-
-        def weighted_pass(g, ch, tag="xt", bufs=3):
-            bank = psum.tile([P, 2, P, PACK], BF16, name=f"wq_{g}_{ch}", tag=tag, bufs=bufs)
-            tiles["wb", g, ch] = bank
-            for s in range(2):
-                c0 = ch * CH + s * P
-                nc.tensor.matmul(
-                    bank[:, s, :, :],
-                    lhsT=ident_b[:],
-                    rhs=tiles["wp", g][:, :, c0 : c0 + P].rearrange("p j n -> p n j"),
-                    start=True,
-                    stop=True,
-                )
-
-        def weighted_exit(g, ch, engine):
-            grouped = work.tile([P, CH, PACK], BF16, name=f"wg_{g}_{ch}", tag="wg", bufs=4, align_bytes=64)
-            tiles["wg", g, ch] = grouped
-            dst = grouped[:].rearrange("p n j -> p (n j)")
-            src = tiles.pop(("wb", g, ch))[:].rearrange("p s n j -> p (s n j)")
+            src = tiles["wp", g][:, :, ch * CH : (ch + 1) * CH].rearrange("p j (n i) -> p n j i", i=4)
+            dst = grouped[:].rearrange("p (n i) j -> p n j i", i=4)
             if engine == "A":
                 nc.scalar.copy(out=dst, in_=src)
             else:
@@ -383,7 +342,11 @@ def tile_cross_impact_hedge_s8_kernel(
         def cost_matmul(qt, half, g):
             if g == 0:
                 bank = psum.tile(
-                    [P, BANK], F32, name=f"cost_{qt}_{half}", tag="xt" if half == 0 else "z", bufs=3 if half == 0 else 2
+                    [P, BANK],
+                    F32,
+                    name=f"cost_{qt}_{half}",
+                    tag="z" if (qt, half) == (1, 1) else "xt",
+                    bufs=2 if (qt, half) == (1, 1) else 3,
                 )
                 tiles["cb", qt, half] = bank
             cols = slice(half * BANK, (half + 1) * BANK)
@@ -407,78 +370,88 @@ def tile_cross_impact_hedge_s8_kernel(
                 nc.vector.tensor_copy(out=dst, in_=src)
             nc.sync.dma_start(out=cost[qt * P : (qt + 1) * P, half * BANK : (half + 1) * BANK], in_=res[:])
 
-        def impact_by_pe(c, half):
-            for b in range(2):
-                impact_pass(c, half, b)
-                impact_exit(c, half, b, "A")
-
         spread_scale()
         impact_interleave(0, 0, "D")
-        impact_by_pe(1, 0)
-        widen(0)
+        impact_interleave(1, 0, "D")
+        impact_interleave(2, 0, "A")
         impact_quantize(0, 0)
-        impact_by_pe(2, 0)
+        widen(0)
         flow_transpose(0)
         flow_exit(0)
-        impact_quantize(1, 0)
-        impact_by_pe(0, 1)
+        impact_interleave(0, 1, "A")
         widen(1)
         impact_quantize(2, 0)
-        flow_quantize(0)
-        impact_by_pe(1, 1)
+        impact_quantize(1, 0)
         flow_transpose(1)
+        flow_quantize(0)
         flow_exit(1)
-        impact_quantize(0, 1)
+        impact_interleave(1, 1, "A")
+        widen(2)
         impact_matmul(0, 0)
         saturate(0, 0)
-        impact_by_pe(2, 1)
-        impact_quantize(1, 1)
-        widen(2)
         flow_quantize(1)
-        impact_quantize(2, 1)
+        impact_quantize(0, 1)
+        impact_matmul(1, 0)
+        flow_transpose(2)
+        flow_exit(2)
+        saturate(1, 0)
+        moves_transpose(0, 0)
+        widen(3)
+        impact_interleave(2, 1, "D")
+        impact_quantize(1, 1)
         nc.vector.tensor_copy(out=vol_f[:], in_=vol_b[:])
         nc.vector.tensor_copy(out=depth_f[:], in_=depth_b[:])
+        impact_quantize(2, 1)
+        moves_scale(0, 0)
         impact_matmul(0, 1)
         saturate(0, 1)
+        widen(4)
+        flow_quantize(2)
 
+        early = [(0, 0, 0), (1, 0, 0), (0, 0, 1), (1, 0, 1), (0, 0, 2), (1, 0, 2), (0, 1, 0), (0, 1, 1)]
+
+        def cost_early(count):
+            for c in range(count):
+                qt, half, g2 = early.pop(0)
+                cost_matmul(qt, half, g2)
+
+        chunk_step = (7, 8, 9, 10, 11, 12, 12, 13, 13, 14, 15, 15)
         for s in range(1, TILES):
-            g, ch = divmod(s - PACK, CHUNKS)
+            chunks = [k for k in range(len(chunk_step)) if chunk_step[k] == s]
             if s + W_LEAD < TILES:
                 widen(s + W_LEAD)
             if s >= 3:
                 hedge_exit(s - 3, "A")
-            if s + 1 < TILES:
-                flow_transpose(s + 1)
-                flow_exit(s + 1)
+            if s + 2 < TILES:
+                flow_transpose(s + 2)
+                flow_exit(s + 2)
             weigh(s - 1, "A")
-            if 3 <= s < 7:
-                sched_transpose(s - 3)
-                sched_exit(s - 3)
+            if 9 <= s < 9 + 4:
+                sched_transpose(s - 9)
+                sched_exit(s - 9)
+            if s >= TILES - 2:
+                cost_early(2)
             for half in range(N_PASSES):
-                moves_transpose(s - 1, half)
-                moves_scale(s - 1, half)
-            if s + 1 < TILES:
-                flow_quantize(s + 1)
-            if s >= PACK:
-                if ch % 2 == 1:
-                    weighted_pass(g, ch)
-                    weighted_exit(g, ch, "A")
-                else:
-                    weighted_interleave(g, ch, "D")
+                if (s - 1, half) not in ((0, 0),):
+                    moves_transpose(s - 1, half)
+                    moves_scale(s - 1, half)
+                    if s >= TILES - 2:
+                        cost_early(1)
+            if s + 2 < TILES:
+                flow_quantize(s + 2)
+            for k in chunks:
+                weighted_interleave(k // CHUNKS, k % CHUNKS, "A" if k in () else "D")
             moves_quantize(s - 1)
-            if 3 <= s < 7:
-                sched_quantize(s - 3)
+            if 9 <= s < 9 + 4:
+                sched_quantize(s - 9)
             if s >= 2:
                 hedge_matmul(s - 2)
-            if s >= PACK:
-                weighted_quantize(g, ch)
-            if s == TILES - 1:
-                for g2 in range(T_PASSES - 1):
-                    for qt in range(2):
-                        cost_matmul(qt, 0, g2)
+            for k in chunks:
+                weighted_quantize(k // CHUNKS, k % CHUNKS)
             for half in range(N_PASSES):
-                impact_matmul(s, half)
-                saturate(s, half)
+                if (s, half) not in ((1, 0),):
+                    impact_matmul(s, half)
+                    saturate(s, half)
 
         last = TILES - 1
         g = T_PASSES - 1
@@ -486,8 +459,7 @@ def tile_cross_impact_hedge_s8_kernel(
         hedge_exit(last - 2, "A")
         moves_transpose(last, 0)
         weighted_interleave(g, 0, "D")
-        weighted_pass(g, 1)
-        weighted_exit(g, 1, "A")
+        weighted_interleave(g, 1, "A")
         moves_scale(last, 0)
         weigh(last, "D", BANK, N)
         moves_transpose(last, 1)
@@ -495,13 +467,12 @@ def tile_cross_impact_hedge_s8_kernel(
         weighted_quantize(g, 0)
         moves_scale(last, 1)
         hedge_exit(last - 1, "A")
+        cost_matmul(0, 1, T_PASSES - 2)
         for g2 in range(T_PASSES - 1):
-            for qt in range(2):
-                cost_matmul(qt, 1, g2)
+            cost_matmul(1, 1, g2)
         weighted_quantize(g, 1)
         weighted_interleave(g, 2, "D")
-        weighted_pass(g, 3, "ht", 2)
-        weighted_exit(g, 3, "A")
+        weighted_interleave(g, 3, "A")
         moves_quantize(last)
         for qt in range(2):
             cost_matmul(qt, 0, g)

@@ -256,7 +256,7 @@ def tile_cross_impact_hedge_s8_kernel(
             )
 
         def moves_transpose(i, half):
-            bank = psum.tile([P, PACK, P], F32, name=f"ht_{i}_{half}", tag="ht", bufs=2)
+            bank = psum.tile([P, PACK, P], F32, name=f"ht_{i}_{half}", tag="z" if i == TILES - 1 else "ht", bufs=2)
             tiles["ht", i, half] = bank
             h = tiles["h", i]
             for j in range(PACK):
@@ -287,7 +287,8 @@ def tile_cross_impact_hedge_s8_kernel(
 
         def hedge_matmul(i):
             codes, scales = tiles.pop(("mc", i))
-            bank = psum.tile([P, R], F32, name=f"hg_{i}", tag="hg", bufs=1)
+            side = i in (TILES - 3, TILES - 1)
+            bank = psum.tile([P, R], F32, name=f"hg_{i}", tag="ht" if side else "hg", bufs=2 if side else 1)
             tiles["hg", i] = bank
             for g in range(N_PASSES):
                 nc.tensor.matmul_mx(
@@ -345,7 +346,7 @@ def tile_cross_impact_hedge_s8_kernel(
                     [P, BANK],
                     F32,
                     name=f"cost_{qt}_{half}",
-                    tag="z" if (qt, half) == (1, 1) else "xt",
+                    tag="ht" if (qt, half) == (1, 1) else "xt",
                     bufs=2 if (qt, half) == (1, 1) else 3,
                 )
                 tiles["cb", qt, half] = bank
@@ -379,9 +380,9 @@ def tile_cross_impact_hedge_s8_kernel(
         flow_transpose(0)
         flow_exit(0)
         impact_interleave(0, 1, "A")
+        impact_quantize(1, 0)
         widen(1)
         impact_quantize(2, 0)
-        impact_quantize(1, 0)
         flow_transpose(1)
         flow_quantize(0)
         flow_exit(1)
@@ -395,92 +396,102 @@ def tile_cross_impact_hedge_s8_kernel(
         flow_transpose(2)
         flow_exit(2)
         saturate(1, 0)
-        moves_transpose(0, 0)
         widen(3)
         impact_interleave(2, 1, "D")
         impact_quantize(1, 1)
         nc.vector.tensor_copy(out=vol_f[:], in_=vol_b[:])
         nc.vector.tensor_copy(out=depth_f[:], in_=depth_b[:])
         impact_quantize(2, 1)
-        moves_scale(0, 0)
+        flow_transpose(3)
+        flow_exit(3)
         impact_matmul(0, 1)
-        saturate(0, 1)
         widen(4)
         flow_quantize(2)
 
-        early = [(0, 0, 0), (1, 0, 0), (0, 0, 1), (1, 0, 1), (0, 0, 2), (1, 0, 2), (0, 1, 0), (0, 1, 1)]
+        early = [(0, 0, 0), (1, 0, 0), (0, 1, 0), (0, 0, 1), (1, 0, 1), (0, 1, 1), (0, 0, 2), (1, 0, 2), (0, 1, 2)]
 
         def cost_early(count):
             for c in range(count):
-                qt, half, g2 = early.pop(0)
-                cost_matmul(qt, half, g2)
+                cost_matmul(*early.pop(0))
 
-        chunk_step = (7, 8, 9, 10, 11, 12, 12, 13, 13, 14, 15, 15)
+        on_scalar = (0, 3, 6,)
+        chunk_step = (5, 6, 7, 8, 9, 10, 11, 12, 13, 14, 14, 15)
         for s in range(1, TILES):
             chunks = [k for k in range(len(chunk_step)) if chunk_step[k] == s]
-            if s + W_LEAD < TILES:
-                widen(s + W_LEAD)
-            if s >= 3:
-                hedge_exit(s - 3, "A")
-            if s + 2 < TILES:
+            if 0 <= s - 3 < TILES:
+                moves_quantize(s - 3)
+            for half in range(N_PASSES):
+                if (s - 1, half) not in ((0, 0), (1, 0)):
+                    saturate(s - 1, half)
+            if 4 <= s + 2 < TILES:
                 flow_transpose(s + 2)
                 flow_exit(s + 2)
+            if 3 <= s + 1 < TILES:
+                flow_quantize(s + 1)
             weigh(s - 1, "A")
             if 9 <= s < 9 + 4:
                 sched_transpose(s - 9)
                 sched_exit(s - 9)
             if s >= TILES - 2:
-                cost_early(2)
+                cost_early(2 if s == TILES - 2 else 2)
             for half in range(N_PASSES):
-                if (s - 1, half) not in ((0, 0),):
-                    moves_transpose(s - 1, half)
-                    moves_scale(s - 1, half)
-                    if s >= TILES - 2:
-                        cost_early(1)
-            if s + 2 < TILES:
-                flow_quantize(s + 2)
+                if s >= 2 and (s - 2, half) not in ():
+                    moves_transpose(s - 2, half)
+                    moves_scale(s - 2, half)
             for k in chunks:
-                weighted_interleave(k // CHUNKS, k % CHUNKS, "A" if k in () else "D")
-            moves_quantize(s - 1)
+                weighted_interleave(k // CHUNKS, k % CHUNKS, "A" if k in on_scalar else "D")
             if 9 <= s < 9 + 4:
                 sched_quantize(s - 9)
-            if s >= 2:
-                hedge_matmul(s - 2)
+            if s >= 4:
+                hedge_matmul(s - 4)
+                hedge_exit(s - 4, "A")
+            if 5 <= s + 4 < TILES:
+                widen(s + 4)
             for k in chunks:
                 weighted_quantize(k // CHUNKS, k % CHUNKS)
             for half in range(N_PASSES):
                 if (s, half) not in ((1, 0),):
                     impact_matmul(s, half)
-                    saturate(s, half)
 
         last = TILES - 1
         g = T_PASSES - 1
+        saturate(last, 0)
         weigh(last, "D", 0, BANK)
-        hedge_exit(last - 2, "A")
-        moves_transpose(last, 0)
-        weighted_interleave(g, 0, "D")
+        saturate(last, 1)
+        moves_quantize(last - 2)
+        for i in (last - 1, last):
+            for half in range(N_PASSES):
+                moves_transpose(i, half)
         weighted_interleave(g, 1, "A")
-        moves_scale(last, 0)
+        moves_scale(last - 1, 0)
         weigh(last, "D", BANK, N)
-        moves_transpose(last, 1)
-        hedge_matmul(last - 1)
+        moves_scale(last - 1, 1)
+        hedge_matmul(last - 3)
+        hedge_exit(last - 3, "A")
+        weighted_interleave(g, 0, "D")
+        moves_scale(last, 0)
+        moves_quantize(last - 1)
+        hedge_matmul(last - 2)
+        weighted_interleave(g, 3, "A")
+        hedge_exit(last - 2, "A")
+        cost_early(len(early))
         weighted_quantize(g, 0)
         moves_scale(last, 1)
-        hedge_exit(last - 1, "A")
-        cost_matmul(0, 1, T_PASSES - 2)
-        for g2 in range(T_PASSES - 1):
-            cost_matmul(1, 1, g2)
         weighted_quantize(g, 1)
         weighted_interleave(g, 2, "D")
-        weighted_interleave(g, 3, "A")
-        moves_quantize(last)
+        hedge_matmul(last - 1)
+        hedge_exit(last - 1, "A")
+        for g2 in range(T_PASSES - 1):
+            cost_matmul(1, 1, g2)
         for qt in range(2):
             cost_matmul(qt, 0, g)
             cost_exit(qt, 0, "A")
-        hedge_matmul(last)
-        hedge_exit(last, "A")
+        moves_quantize(last)
         weighted_quantize(g, 2)
         weighted_quantize(g, 3)
+        hedge_matmul(last)
         for qt in range(2):
             cost_matmul(qt, 1, g)
-            cost_exit(qt, 1, "A" if qt == 0 else "D")
+        hedge_exit(last, "A")
+        cost_exit(0, 1, "D")
+        cost_exit(1, 1, "D")

from contextlib import ExitStack

import concourse.mybir as mybir
from concourse.masks import make_identity

T, A, N, R, Q = 2048, 1536, 1024, 512, 256

F32 = mybir.dt.float32
BF16 = mybir.dt.bfloat16
U8 = mybir.dt.uint8
U32 = mybir.dt.uint32
I32 = mybir.dt.int32
FP8 = mybir.dt.float8_e4m3fn
FP8X4 = mybir.dt.float8_e4m3fn_x4
FP4X4 = mybir.dt.float4_e2m1fn_x4
MULT = mybir.AluOpType.mult
TANH = mybir.ActivationFunctionType.Tanh
COPY = mybir.ActivationFunctionType.Copy

FLOPS = 2 * T * A * N + 2 * T * N * R + 2 * Q * T * N

P = 128
PACK = 4
K_PASS = P * PACK
A_PASSES = A // K_PASS
N_PASSES = N // K_PASS
T_PASSES = T // K_PASS
TILES = T // P
BANK = 512
W_LEAD = 4
CH = 256
CHUNKS = N // CH


def tile_cross_impact_hedge_s8_kernel(
    tc, flow_bytes, flow_scale, impact, vol, depth, sched, sens_words, sens_scales, hedge, cost
):
    nc = tc.nc
    with ExitStack() as ctx:
        keep = ctx.enter_context(tc.tile_pool(name="keep", bufs=1))
        work = ctx.enter_context(tc.tile_pool(name="work", bufs=3))
        psum = ctx.enter_context(tc.psum_pool(name="psum", bufs=2))
        ctx.enter_context(tc.manual_schedule())

        warm = keep.tile([P, 1], F32, name="warm")
        nc.vector.memset(warm[:], 0.0)
        nc.scalar.activation(out=warm[:], in_=warm[:], func=TANH)
        scale_rows = keep.tile([P, 3 * P], F32, name="scale_rows")
        nc.vector.memset(scale_rows[:], 0.0)
        w_scales = keep.tile([P, N_PASSES, R], U8, name="w_scales", align_bytes=64)
        nc.vector.memset(w_scales[:].bitcast(I32), 0)
        ident = keep.tile([P, P], F32, name="ident")
        make_identity(nc, ident[:])

        flow_view = flow_bytes.rearrange("(g p j) a -> g p j a", p=P, j=PACK)
        flow_sb = []
        for g in range(T_PASSES):
            for half in range(2):
                t_f = keep.tile([P, 2, A], U8, name=f"flow_{g}_{half}", align_bytes=64)
                flow_sb.append(t_f)

        def load_flow(pair):
            g, half = divmod(pair, 2)
            nc.sync.dma_start(out=flow_sb[pair][:], in_=flow_view[g, :, 2 * half : 2 * half + 2, :])

        imp_view = impact.rearrange("(c p t) n -> c p t n", p=P, t=PACK)
        imp_raw = {}
        for c in range(A_PASSES):
            for half in range(N_PASSES):
                t_i = keep.tile([P, PACK, BANK], BF16, name=f"imp_raw_{c}_{half}", align_bytes=64)
                imp_raw[c, half] = t_i

        def load_impact(c, half):
            nc.sync.dma_start(out=imp_raw[c, half][:], in_=imp_view[c, :, :, half * BANK : (half + 1) * BANK])

        scale_sb = keep.tile([P, A], F32, name="scale_sb", align_bytes=64)
        vol_b = keep.tile([P, N_PASSES, PACK], BF16, name="vol_b")
        depth_b = keep.tile([P, T_PASSES, PACK], BF16, name="depth_b")
        w_words = keep.tile([P, N_PASSES, 2 * R], U8, name="w_words", align_bytes=64)
        sched_sb = []
        for qt in range(2):
            t_s = keep.tile([P, T], BF16, name=f"sched_{qt}", align_bytes=64)
            sched_sb.append(t_s)

        nc.sync.dma_start(out=scale_rows[0:4, :], in_=flow_scale.rearrange("o (r k) -> (o r) k", r=4))
        load_impact(0, 0)
        load_impact(1, 0)
        load_flow(0)
        load_impact(2, 0)
        load_impact(0, 1)
        load_impact(1, 1)
        load_impact(2, 1)
        load_flow(1)
        load_flow(2)
        nc.sync.dma_start(out=vol_b[:], in_=vol.rearrange("(g p j) -> p g j", p=P, j=PACK))
        nc.sync.dma_start(out=depth_b[:], in_=depth.rearrange("(g p j) -> p g j", p=P, j=PACK))
        for q4 in range(4):
            nc.sync.dma_start(
                out=w_scales[32 * q4 : 32 * q4 + 4, :, :].bitcast(I32),
                in_=sens_scales[:, 4 * q4 : 4 * q4 + 4, :].rearrange("g r n -> r g n").bitcast(I32),
            )
        nc.sync.dma_start(out=w_words[:].bitcast(I32), in_=sens_words.rearrange("g p b -> p g b").bitcast(I32))
        load_flow(3)
        load_flow(4)
        for qt in range(2):
            nc.sync.dma_start(out=sched_sb[qt][:], in_=sched[qt * P : (qt + 1) * P, :])
        load_flow(5)
        load_flow(6)
        load_flow(7)

        vol_f = keep.tile([P, N_PASSES, PACK], F32, name="vol_f")
        depth_f = keep.tile([P, T_PASSES, PACK], F32, name="depth_f")

        imp_codes = keep.tile([P, A_PASSES, N], U32, name="imp_codes", align_bytes=64)
        imp_scales = keep.tile([P, A_PASSES, N], U8, name="imp_scales", align_bytes=64)
        wt_codes = keep.tile([P, T_PASSES, N], U32, name="wt_codes", align_bytes=64)
        wt_scales = keep.tile([P, T_PASSES, N], U8, name="wt_scales", align_bytes=64)
        sch_codes = keep.tile([P, 2, T_PASSES, P], U32, name="sch_codes", align_bytes=64)
        sch_scales = keep.tile([P, 2, T_PASSES, P], U8, name="sch_scales", align_bytes=64)
        tiles = {}

        def impact_interleave(c, half, engine):
            grouped = work.tile([P, BANK, PACK], BF16, name=f"imp_grp_{c}_{half}", tag="imp_grp", bufs=3, align_bytes=64)
            tiles["ig", c, half] = grouped
            dst = grouped[:].rearrange("p (n i) t -> p n t i", i=4)
            src = imp_raw[c, half][:].rearrange("p t (n i) -> p n t i", i=4)
            if engine == "A":
                nc.scalar.copy(out=dst, in_=src)
            else:
                nc.vector.tensor_copy(out=dst, in_=src)

        def impact_quantize(c, half):
            cols = slice(half * BANK, (half + 1) * BANK)
            nc.vector.quantize_mx(
                out=imp_codes[:, c, cols].bitcast(FP8X4),
                scales=imp_scales[:, c, cols],
                in_=tiles.pop(("ig", c, half))[:].rearrange("p n t -> p (n t)"),
            )

        def spread_scale():
            bank = psum.tile([P, 3, P], F32, name="scale_cols", tag="ht", bufs=2)
            for b in range(3):
                nc.tensor.transpose(bank[:, b, :], scale_rows[:, b * P : (b + 1) * P], ident[:])
            scale_cols = keep.tile([P, 4, 3], F32, name="scale_cols_sb")
            nc.scalar.copy(out=scale_cols[:], in_=bank[:, :, 0:4].rearrange("p b r -> p r b"))
            for c in range(A_PASSES):
                bank = psum.tile([P, PACK, P], F32, name=f"scale_bank_{c}", tag="z", bufs=2)
                for s in range(PACK):
                    k = PACK * c + s
                    nc.tensor.transpose(
                        bank[:, s, :], scale_cols[:, k // 3, k % 3 : k % 3 + 1].to_broadcast([P, P]), ident[:]
                    )
                nc.scalar.copy(
                    out=scale_sb[:, c * K_PASS : (c + 1) * K_PASS], in_=bank[:].rearrange("p s k -> p (s k)")
                )

        def widen(i):
            wide = work.tile([P, A], BF16, name=f"wide_{i}", tag="wide", bufs=5, align_bytes=64)
            tiles["wide", i] = wide
            nc.vector.tensor_tensor(
                out=wide[:], in0=flow_sb[i // 2][:, i % 2, :].bitcast(FP8), in1=scale_sb[:], op=MULT
            )

        def flow_transpose(i):
            words = tiles.pop(("wide", i))[:].bitcast(F32)
            for part, passes in ((0, (0, 1)), (1, (2,))):
                bank = psum.tile([P, PACK, P], F32, name=f"xt_{i}_{part}", tag="xt", bufs=3)
                tiles["xt", i, part] = bank
                slot = 0
                for c in passes:
                    for u in range(2):
                        nc.tensor.transpose(
                            bank[:, slot, :], words[:, 256 * c + u : 256 * (c + 1) : 2], ident[:]
                        )
                        slot += 1

        def flow_exit(i):
            grouped = work.tile([P, A_PASSES, P, PACK], BF16, name=f"fg_{i}", tag="fg", bufs=3, align_bytes=64)
            tiles["fg", i] = grouped
            words = grouped[:].rearrange("p c r t -> p (c r t)").bitcast(F32)
            words = words.rearrange("p (c r u) -> p c r u", c=A_PASSES, u=2)
            xt0 = tiles.pop(("xt", i, 0))
            xt1 = tiles.pop(("xt", i, 1))
            nc.scalar.copy(out=words[:, 0:2, :, :], in_=xt0[:].rearrange("p (c u) r -> p c r u", u=2))
            nc.scalar.copy(out=words[:, 2, :, :], in_=xt1[:, 0:2, :].rearrange("p u r -> p r u"))

        def flow_quantize(i):
            codes = work.tile([P, A_PASSES, P], U32, name=f"fc_{i}", tag="fc", bufs=4, align_bytes=64)
            scales = work.tile([P, A_PASSES, P], U8, name=f"fs_{i}", tag="fs", bufs=4, align_bytes=64)
            tiles["fc", i] = (codes, scales)
            grouped = tiles.pop(("fg", i))
            for lo, hi in ((0, 2), (2, 3)):
                nc.vector.quantize_mx(
                    out=codes[:, lo:hi, :].rearrange("p c r -> p (c r)").bitcast(FP8X4),
                    scales=scales[:, lo:hi, :].rearrange("p c r -> p (c r)"),
                    in_=grouped[:, lo:hi, :, :].rearrange("p c r t -> p (c r t)"),
                )

        def impact_matmul(i, half):
            codes, scales = tiles["fc", i]
            z = psum.tile([P, BANK], F32, name=f"z_{i}_{half}", tag="z", bufs=2)
            tiles["z", i, half] = z
            cols = slice(half * BANK, (half + 1) * BANK)
            for c in range(A_PASSES):
                nc.tensor.matmul_mx(
                    out=z[:],
                    lhsT=codes[:, c, :].bitcast(FP8X4),
                    lhsT_scale=scales[:, c, :],
                    rhs=imp_codes[:, c, cols].bitcast(FP8X4),
                    rhs_scale=imp_scales[:, c, cols],
                    start=(c == 0),
                    stop=(c == A_PASSES - 1),
                )

        def saturate(i, half):
            if half == 0:
                h = work.tile([P, N], F32, name=f"h_{i}", tag="h", bufs=4, align_bytes=64)
                tiles["h", i] = h
            nc.scalar.activation(
                out=tiles["h", i][:, half * BANK : (half + 1) * BANK].rearrange("p (j m) -> p j m", j=PACK),
                in_=tiles.pop(("z", i, half))[:].rearrange("p (m j) -> p j m", j=PACK),
                func=TANH,
            )

        def weigh(i, engine, lo=0, hi=N):
            g, j = divmod(i, PACK)
            if j == 0:
                planes = work.tile([P, PACK, N], BF16, name=f"wp_{g}", tag="wp", bufs=3, align_bytes=64)
                tiles["wp", g] = planes
            planes = tiles["wp", g]
            if engine == "A":
                nc.scalar.activation(
                    out=planes[:, j, lo:hi], in_=tiles["h", i][:, lo:hi], func=COPY, scale=depth_f[:, g, j : j + 1]
                )
            else:
                nc.vector.tensor_scalar(
                    out=planes[:, j, lo:hi], in0=tiles["h", i][:, lo:hi], scalar1=depth_f[:, g, j : j + 1], scalar2=None, op0=MULT
                )

        def weighted_interleave(g, ch, engine):
            grouped = work.tile([P, CH, PACK], BF16, name=f"wg_{g}_{ch}", tag="wg", bufs=4, align_bytes=64)
            tiles["wg", g, ch] = grouped
            src = tiles["wp", g][:, :, ch * CH : (ch + 1) * CH].rearrange("p j (n i) -> p n j i", i=4)
            dst = grouped[:].rearrange("p (n i) j -> p n j i", i=4)
            if engine == "A":
                nc.scalar.copy(out=dst, in_=src)
            else:
                nc.vector.tensor_copy(out=dst, in_=src)

        def weighted_quantize(g, ch):
            cols = slice(ch * CH, (ch + 1) * CH)
            nc.vector.quantize_mx(
                out=wt_codes[:, g, cols].bitcast(FP8X4),
                scales=wt_scales[:, g, cols],
                in_=tiles.pop(("wg", g, ch))[:].rearrange("p n t -> p (n t)"),
            )

        def moves_transpose(i, half):
            bank = psum.tile([P, PACK, P], F32, name=f"ht_{i}_{half}", tag="z" if i == TILES - 1 else "ht", bufs=2)
            tiles["ht", i, half] = bank
            h = tiles["h", i]
            for j in range(PACK):
                c0 = half * BANK + j * P
                nc.tensor.transpose(bank[:, j, :], h[:, c0 : c0 + P], ident[:])

        def moves_scale(i, half):
            if half == 0:
                grouped = work.tile([P, N_PASSES, P, PACK], BF16, name=f"mg_{i}", tag="mg", bufs=3, align_bytes=64)
                tiles["mg", i] = grouped
            grouped = tiles["mg", i]
            nc.vector.tensor_tensor(
                out=grouped[:, half, :, :],
                in0=tiles.pop(("ht", i, half))[:].rearrange("p j t -> p t j"),
                in1=vol_f[:, half, :].unsqueeze(1).to_broadcast([P, P, PACK]),
                op=MULT,
            )

        def moves_quantize(i):
            codes = work.tile([P, N_PASSES, P], U32, name=f"mc_{i}", tag="mc", bufs=4, align_bytes=64)
            scales = work.tile([P, N_PASSES, P], U8, name=f"ms_{i}", tag="ms", bufs=4, align_bytes=64)
            tiles["mc", i] = (codes, scales)
            nc.vector.quantize_mx(
                out=codes[:].rearrange("p g t -> p (g t)").bitcast(FP8X4),
                scales=scales[:].rearrange("p g t -> p (g t)"),
                in_=tiles.pop(("mg", i))[:].rearrange("p g t j -> p (g t j)"),
            )

        def hedge_matmul(i):
            codes, scales = tiles.pop(("mc", i))
            side = i in (TILES - 3, TILES - 1)
            bank = psum.tile([P, R], F32, name=f"hg_{i}", tag="ht" if side else "hg", bufs=2 if side else 1)
            tiles["hg", i] = bank
            for g in range(N_PASSES):
                nc.tensor.matmul_mx(
                    out=bank[:],
                    lhsT=codes[:, g, :].bitcast(FP8X4),
                    lhsT_scale=scales[:, g, :],
                    rhs=w_words[:, g, :].bitcast(FP4X4),
                    rhs_scale=w_scales[:, g, :],
                    start=(g == 0),
                    stop=(g == N_PASSES - 1),
                )

        hedge_view = hedge.rearrange("(g p j) r -> g j p r", p=P, j=PACK)

        def hedge_exit(i, engine):
            g, j = divmod(i, PACK)
            res = work.tile([P, R], F32, name=f"hr_{i}", tag="hr", bufs=3, align_bytes=64)
            bank = tiles.pop(("hg", i))
            if engine == "A":
                nc.scalar.copy(out=res[:], in_=bank[:])
            else:
                nc.vector.tensor_copy(out=res[:], in_=bank[:])
            nc.sync.dma_start(out=hedge_view[g, j], in_=res[:])

        def sched_transpose(b):
            qt, gp = divmod(b, 2)
            words = sched_sb[qt][:].bitcast(F32)
            bank = psum.tile([P, PACK, P], F32, name=f"st_{b}", tag="xt", bufs=3)
            tiles["st", b] = bank
            for s in range(2):
                g = 2 * gp + s
                for u in range(2):
                    nc.tensor.transpose(bank[:, 2 * s + u, :], words[:, 256 * g + u : 256 * (g + 1) : 2], ident[:])

        def sched_exit(b):
            grouped = work.tile([P, 2, P, PACK], BF16, name=f"sg_{b}", tag="sg", bufs=2, align_bytes=64)
            tiles["sg", b] = grouped
            words = grouped[:].rearrange("p s q t -> p (s q t)").bitcast(F32)
            nc.scalar.copy(
                out=words.rearrange("p (s q u) -> p s q u", s=2, u=2),
                in_=tiles.pop(("st", b))[:].rearrange("p (s u) q -> p s q u", u=2),
            )

        def sched_quantize(b):
            qt, gp = divmod(b, 2)
            nc.vector.quantize_mx(
                out=sch_codes[:, qt, 2 * gp : 2 * gp + 2, :].rearrange("p s q -> p (s q)").bitcast(FP8X4),
                scales=sch_scales[:, qt, 2 * gp : 2 * gp + 2, :].rearrange("p s q -> p (s q)"),
                in_=tiles.pop(("sg", b))[:].rearrange("p s q t -> p (s q t)"),
            )

        def cost_matmul(qt, half, g):
            if g == 0:
                bank = psum.tile(
                    [P, BANK],
                    F32,
                    name=f"cost_{qt}_{half}",
                    tag="ht" if (qt, half) == (1, 1) else "xt",
                    bufs=2 if (qt, half) == (1, 1) else 3,
                )
                tiles["cb", qt, half] = bank
            cols = slice(half * BANK, (half + 1) * BANK)
            nc.tensor.matmul_mx(
                out=tiles["cb", qt, half][:],
                lhsT=sch_codes[:, qt, g, :].bitcast(FP8X4),
                lhsT_scale=sch_scales[:, qt, g, :],
                rhs=wt_codes[:, g, cols].bitcast(FP8X4),
                rhs_scale=wt_scales[:, g, cols],
                start=(g == 0),
                stop=(g == T_PASSES - 1),
            )

        def cost_exit(qt, half, engine):
            res = work.tile([P, BANK], F32, name=f"cr_{qt}_{half}", tag="cr", bufs=4, align_bytes=64)
            dst = res[:].rearrange("p (m j) -> p m j", j=PACK)
            src = tiles.pop(("cb", qt, half))[:].rearrange("p (j m) -> p m j", j=PACK)
            if engine == "A":
                nc.scalar.copy(out=dst, in_=src)
            else:
                nc.vector.tensor_copy(out=dst, in_=src)
            nc.sync.dma_start(out=cost[qt * P : (qt + 1) * P, half * BANK : (half + 1) * BANK], in_=res[:])

        spread_scale()
        impact_interleave(0, 0, "D")
        impact_interleave(1, 0, "D")
        impact_interleave(2, 0, "A")
        impact_quantize(0, 0)
        widen(0)
        flow_transpose(0)
        flow_exit(0)
        impact_interleave(0, 1, "A")
        impact_quantize(1, 0)
        widen(1)
        impact_quantize(2, 0)
        flow_transpose(1)
        flow_quantize(0)
        flow_exit(1)
        impact_interleave(1, 1, "A")
        widen(2)
        impact_matmul(0, 0)
        saturate(0, 0)
        flow_quantize(1)
        impact_quantize(0, 1)
        impact_matmul(1, 0)
        flow_transpose(2)
        flow_exit(2)
        saturate(1, 0)
        widen(3)
        impact_interleave(2, 1, "D")
        impact_quantize(1, 1)
        nc.vector.tensor_copy(out=vol_f[:], in_=vol_b[:])
        nc.vector.tensor_copy(out=depth_f[:], in_=depth_b[:])
        impact_quantize(2, 1)
        flow_transpose(3)
        flow_exit(3)
        impact_matmul(0, 1)
        widen(4)
        flow_quantize(2)

        early = [(0, 0, 0), (1, 0, 0), (0, 1, 0), (0, 0, 1), (1, 0, 1), (0, 1, 1), (0, 0, 2), (1, 0, 2), (0, 1, 2)]

        def cost_early(count):
            for c in range(count):
                cost_matmul(*early.pop(0))

        on_scalar = (0, 3, 6,)
        chunk_step = (5, 6, 7, 8, 9, 10, 11, 12, 13, 14, 14, 15)
        for s in range(1, TILES):
            chunks = [k for k in range(len(chunk_step)) if chunk_step[k] == s]
            if 0 <= s - 3 < TILES:
                moves_quantize(s - 3)
            for half in range(N_PASSES):
                if (s - 1, half) not in ((0, 0), (1, 0)):
                    saturate(s - 1, half)
            if 4 <= s + 2 < TILES:
                flow_transpose(s + 2)
                flow_exit(s + 2)
            if 3 <= s + 1 < TILES:
                flow_quantize(s + 1)
            weigh(s - 1, "A")
            if 9 <= s < 9 + 4:
                sched_transpose(s - 9)
                sched_exit(s - 9)
            if s >= TILES - 2:
                cost_early(2 if s == TILES - 2 else 2)
            for half in range(N_PASSES):
                if s >= 2 and (s - 2, half) not in ():
                    moves_transpose(s - 2, half)
                    moves_scale(s - 2, half)
            for k in chunks:
                weighted_interleave(k // CHUNKS, k % CHUNKS, "A" if k in on_scalar else "D")
            if 9 <= s < 9 + 4:
                sched_quantize(s - 9)
            if s >= 4:
                hedge_matmul(s - 4)
                hedge_exit(s - 4, "A")
            if 5 <= s + 4 < TILES:
                widen(s + 4)
            for k in chunks:
                weighted_quantize(k // CHUNKS, k % CHUNKS)
            for half in range(N_PASSES):
                if (s, half) not in ((1, 0),):
                    impact_matmul(s, half)

        last = TILES - 1
        g = T_PASSES - 1
        saturate(last, 0)
        weigh(last, "D", 0, BANK)
        saturate(last, 1)
        moves_quantize(last - 2)
        for i in (last - 1, last):
            for half in range(N_PASSES):
                moves_transpose(i, half)
        weighted_interleave(g, 1, "A")
        moves_scale(last - 1, 0)
        weigh(last, "D", BANK, N)
        moves_scale(last - 1, 1)
        hedge_matmul(last - 3)
        hedge_exit(last - 3, "A")
        weighted_interleave(g, 0, "D")
        moves_scale(last, 0)
        moves_quantize(last - 1)
        hedge_matmul(last - 2)
        weighted_interleave(g, 3, "A")
        hedge_exit(last - 2, "A")
        cost_early(len(early))
        weighted_quantize(g, 0)
        moves_scale(last, 1)
        weighted_quantize(g, 1)
        weighted_interleave(g, 2, "D")
        hedge_matmul(last - 1)
        hedge_exit(last - 1, "A")
        for g2 in range(T_PASSES - 1):
            cost_matmul(1, 1, g2)
        for qt in range(2):
            cost_matmul(qt, 0, g)
            cost_exit(qt, 0, "A")
        moves_quantize(last)
        weighted_quantize(g, 2)
        weighted_quantize(g, 3)
        hedge_matmul(last)
        for qt in range(2):
            cost_matmul(qt, 1, g)
        hedge_exit(last, "A")
        cost_exit(0, 1, "D")
        cost_exit(1, 1, "D")
